import numpy as np
import ml_dtypes


def mxq(x, axis, fmt="e4m3"):
    dtype, down = {"e4m3": (ml_dtypes.float8_e4m3fn, 7), "e5m2": (ml_dtypes.float8_e5m2, 14)}[fmt]
    v = np.moveaxis(np.asarray(x, np.float32).astype(ml_dtypes.bfloat16).astype(np.float64), axis, -1)
    blocks = v.reshape(v.shape[:-1] + (-1, 32))
    amax = np.abs(blocks).max(-1, keepdims=True)
    byte = np.maximum(np.where(amax > 0, np.frexp(amax)[1] - 1 + 127, 0) - down, 1)
    scale = np.exp2(byte - 127.0)
    codes = (blocks / scale).astype(np.float32).astype(dtype).astype(np.float64)
    return np.moveaxis((codes * scale).reshape(v.shape), -1, axis)


WIDE = False


def mx_kscale(k):
    if not WIDE:
        return np.ones(k)
    levels = np.array([10, -10, 5, -5, 0])
    if k % 512:
        return np.exp2(np.random.permutation(np.resize(levels, k // 32))).repeat(32)
    a = np.empty((k // 512, 16))
    for p in range(k // 512):
        a[p, :8] = np.random.permutation(np.resize(levels, 8))
        for g in range(8):
            far = levels[np.abs(levels - a[p, g]) >= 10]
            a[p, g + 8] = far[np.random.randint(len(far))]
    return np.exp2(a.ravel()).repeat(32)


def f64(x):
    return np.asarray(x).astype(np.float64)


def striped(idx):
    return np.tile(idx.reshape(-1, 16).T, (8, 1)).astype(np.uint16)


def unstriped(offs):
    return offs[:16].T.reshape(-1).astype(np.int64)


E2M1 = np.array([0.0, 0.5, 1.0, 1.5, 2.0, 3.0, 4.0, 6.0, -0.0, -0.5, -1.0, -1.5, -2.0, -3.0, -4.0, -6.0])


def pack_weight(w, fmt):
    k, n = w.shape
    w = f64(np.asarray(w, np.float32).astype(ml_dtypes.bfloat16)).reshape(k // 32, 32, n)
    amax = np.abs(w).max(1)
    if fmt == "e4m3":
        byte = np.frexp(amax)[1] - 1 + 127 - 7
    else:
        mant, ex = np.frexp(amax / 6.0)
        byte = np.where(mant > 0.5, ex, ex - 1) + 127
    byte = np.clip(np.where(amax > 0, byte, 1), 1, 254)
    scaled = (w * np.exp2(127.0 - byte)[:, None, :]).reshape(k, n).astype(np.float32)
    by_word = np.ascontiguousarray(scaled.reshape(k // 512, 128, 4, n).transpose(0, 1, 3, 2))
    if fmt == "e4m3":
        words = by_word.astype(ml_dtypes.float8_e4m3fn).view(np.uint8)
    else:
        c = by_word.astype(ml_dtypes.float4_e2m1fn).view(np.uint8) & 0xF
        words = (c[..., 0::2] | (c[..., 1::2] << 4)).reshape(k // 512, 128, 2 * n)
    return np.ascontiguousarray(words), np.ascontiguousarray(byte.astype(np.uint8).reshape(k // 512, 16, n))


def unpack_weight(words, scales, fmt):
    g, _, n = scales.shape
    words = np.ascontiguousarray(words).reshape(g, 128, n, -1)
    if fmt == "e4m3":
        vals = words.view(ml_dtypes.float8_e4m3fn).astype(np.float64)
    else:
        nib = np.empty((g, 128, n, 4), np.uint8)
        nib[..., 0::2] = words & 0xF
        nib[..., 1::2] = words >> 4
        vals = E2M1[nib]
    vals = vals * np.repeat(np.exp2(scales.astype(np.float64) - 127.0), 8, axis=1)[..., None]
    return vals.transpose(0, 1, 3, 2).reshape(g * 512, n)


def gelu(v):
    return 0.5 * v * (1.0 + np.tanh(np.sqrt(2.0 / np.pi) * (v + 0.044715 * v**3)))


K, K2, H, T, S, T2, P = 1024, 512, 1024, 2048, 512, 2048, 1024

def setup_inputs():
    n = np.random.standard_normal
    s, s2, u = mx_kscale(K)[:, None], mx_kscale(K2)[:, None], mx_kscale(H)[:, None]
    perm = np.random.permutation(T2)
    d = {}
    d["tab_words"], d["tab_scales"] = pack_weight(n((K, T)) * s, "e4m3")
    d["offs"] = striped(np.random.permutation(T)[:S])
    d["tab2_words"], d["tab2_scales"] = pack_weight(n((K2, T)) * s2, "e4m3")
    d["offs2"] = striped(np.random.permutation(T)[:S])
    d["offs3"] = striped(perm[:S])
    d["offs4"] = striped(perm[S:2 * S])
    d["offs5"] = striped(np.random.permutation(T2)[:P])
    d["w1"] = ((n((K, H)) / K**0.5 - np.eye(K, H)) / s).astype(np.float32)
    d["w2_words"], d["w2_scales"] = pack_weight(1.4 * n((K2, H)) / K2**0.5 / s2, "e2m1")
    d["b2"] = (0.7 * n(H)).astype(np.float32)
    d["wg1"] = np.exp(0.3 * n((128, S))).astype(np.float32)
    d["wg2"] = np.exp(0.3 * n((128, S))).astype(np.float32)
    d["page0"] = n((H, T2)).astype(np.float32)
    d["gain"] = (np.exp(0.3 * n(H)) * u[:, 0]).astype(np.float32)
    d["w3_words"], d["w3_scales"] = pack_weight(n((H, H)) / H**0.5 / u, "e4m3")
    d["skip"] = (0.8 * np.exp(0.3 * n(H)) / u[:, 0]).astype(np.float32)
    return d

def reference(tab_words, tab_scales, offs, tab2_words, tab2_scales, offs2, offs3, offs4, offs5,
              w1, w2_words, w2_scales, b2, wg1, wg2, page0, gain, w3_words, w3_scales, skip):
    v = unpack_weight(tab_words, tab_scales, "e4m3")[:, unstriped(offs)]
    v2 = unpack_weight(tab2_words, tab2_scales, "e4m3")[:, unstriped(offs2)]
    h1 = np.abs(mxq(f64(w1), 0, "e4m3").T @ v)
    l = (unpack_weight(w2_words, w2_scales, "e2m1").T @ v2) + f64(b2)[:, None]
    h2 = 0.5 * l * (1.0 + np.tanh(0.7978845608 * (l + 0.044715 * l**3)))
    page = f64(page0).copy()
    page[:, unstriped(offs3)] = np.tile(f64(wg1), (H // 128, 1)) * h1
    page[:, unstriped(offs4)] = np.tile(f64(wg2), (H // 128, 1)) * h2
    x = page[:, unstriped(offs5)] * f64(gain)[:, None]
    y = unpack_weight(w3_words, w3_scales, "e4m3").T @ mxq(x, 0, "e4m3")
    return np.square(x * f64(skip)[:, None] - y)

@@ -1,0 +1,281 @@
+from contextlib import ExitStack
+
+import concourse.mybir as mybir
+
+K, K2, H, T, S, T2, M = 1024, 512, 1024, 2048, 512, 2048, 1024
+FLOPS = 2 * (K * H * S + K2 * H * S + H * H * M)
+
+F32 = mybir.dt.float32
+BF16 = mybir.dt.bfloat16
+I32 = mybir.dt.int32
+U32 = mybir.dt.uint32
+U16 = mybir.dt.uint16
+U8 = mybir.dt.uint8
+FP8X4 = mybir.dt.float8_e4m3fn_x4
+FP4X4 = mybir.dt.float4_e2m1fn_x4
+ACT = mybir.ActivationFunctionType
+ALU = mybir.AluOpType
+
+P = 128
+PACK = 4
+KP = P * PACK
+NB = 512
+
+
+def tile_list_throw_board_residual_kernel(
+    tc, tab_words, tab_scales, offs, tab2_words, tab2_scales, offs2, offs3, offs4, offs5,
+    w1, w2_words, w2_scales, b2, wg1, wg2, page0, gain, w3_words, w3_scales, skip, out,
+):
+    nc = tc.nc
+    tiles = [(b, t) for b in range(H // KP) for t in range(PACK)]
+    chunks = M // NB
+
+    with ExitStack() as ctx:
+        keep = ctx.enter_context(tc.tile_pool(name="keep", bufs=1))
+        ring = ctx.enter_context(tc.tile_pool(name="ring", bufs=4))
+        raws = ctx.enter_context(tc.tile_pool(name="raws", bufs=3))
+        psum = ctx.enter_context(tc.psum_pool(name="psum", bufs=1))
+
+        def held(shape, dtype, name):
+            return keep.tile(shape, dtype, name=name, align_bytes=64)
+
+        def load_list(src, name):
+            lst = held(list(src.shape), U16, name)
+            nc.sync.dma_start(lst[:], src)
+            return lst
+
+        def load_words(src, name):
+            words = held([P, src.shape[1]], I32, name)
+            nc.sync.dma_start(words[:], src.rearrange("p c i -> p (c i)").bitcast(I32))
+            return words
+
+        def zeroed_plane(width, name, engine):
+            plane = held([P, width], U8, name)
+            engine.memset(plane[:].bitcast(I32), 0)
+            return plane
+
+        def load_plane(plane, src, queue):
+            passes = src.shape[0]
+            for q in range(4):
+                queue.dma_start(
+                    plane[32 * q : 32 * q + 4 * passes, :].bitcast(I32),
+                    src[:, 4 * q : 4 * q + 4, :].bitcast(I32),
+                )
+
+        def load_rowvec(src, name, queue):
+            vec = held([P, H // KP, PACK], F32, name)
+            queue.dma_start(vec[:], src.rearrange("(b p t) -> p b t", t=PACK, p=P))
+            return vec
+
+        page_rows = page0.rearrange("(b p t) c -> b t p c", t=PACK, p=P)
+        out_rows = out.rearrange("(b p t) m -> b t p m", t=PACK, p=P)
+        pages = {}
+
+        def load_page(j):
+            b, t = tiles[j]
+            pages[j] = held([P, T2], F32, "page%d" % j)
+            nc.sync.dma_start(pages[j][:], page_rows[b, t])
+
+        def load_gate(src, t0, t1, name, queue):
+            gate = held([P, t1 - t0, S], F32, name)
+            rows = src.rearrange("(q t) s -> q t s", t=PACK)
+            for q in range(4):
+                queue.dma_start(gate[32 * q : 32 * q + 32], rows[:, t0:t1, :])
+            return gate
+
+        def deal_columns(dst, src):
+            nc.vector.tensor_copy(
+                dst.rearrange("p (b t q) -> p b q t", t=PACK, q=P),
+                src.rearrange("p (b q t) -> p b q t", t=PACK, q=P),
+            )
+
+        def gather(dst, window, offsets):
+            nc.vector.tensor_copy(dst, window.indirect(offsets))
+
+        tab2_plane = zeroed_plane(T, "tab2_plane", nc.gpsimd)
+        w2_plane_raw = zeroed_plane(H, "w2_plane_raw", nc.gpsimd)
+        warm = held([P, 1], F32, "warm")
+        nc.vector.memset(warm[:], 0.0)
+        nc.scalar.activation(warm[:], warm[:], ACT.Gelu_apprx_tanh)
+
+        list2 = load_list(offs2, "list2")
+        load_plane(tab2_plane, tab2_scales, nc.sync)
+        w2_raw = held([P, H // 2], I32, "w2_raw")
+        nc.sync.dma_start(w2_raw[:], w2_words[0].bitcast(I32))
+        tab2_sb = load_words(tab2_words[0], "tab2_sb")
+        load_page(0)
+        load_plane(w2_plane_raw, w2_scales, nc.scalar)
+        b2_sb = load_rowvec(b2, "b2_sb", nc.scalar)
+        list4 = load_list(offs4, "list4")
+        gate2_first = load_gate(wg2, 0, 1, "gate2_first", nc.gpsimd)
+        load_page(1)
+        gate2_rest = load_gate(wg2, 1, PACK, "gate2_rest", nc.sync)
+        load_page(2)
+        load_page(3)
+
+        tab_plane = zeroed_plane(T, "tab_plane", nc.vector)
+        w3_plane_raw = zeroed_plane(H, "w3_plane_raw", nc.vector)
+        list1 = load_list(offs, "list1")
+        load_plane(tab_plane, tab_scales, nc.sync)
+        tab_sb = [load_words(tab_words[a], "tab_sb%d" % a) for a in range(K // KP)]
+        load_page(4)
+
+        w1_raw = {}
+
+        def load_w1(a, b):
+            w1_raw[a, b] = raws.tile([P, PACK, KP], F32, name="raw")
+            nc.sync.dma_start(
+                w1_raw[a, b][:],
+                w1[KP * a : KP * (a + 1), KP * b : KP * (b + 1)].rearrange("(p j) c -> p j c", j=PACK),
+            )
+
+        load_w1(0, 0)
+        load_w1(1, 0)
+        load_page(5)
+        list3 = load_list(offs3, "list3")
+        list5 = load_list(offs5, "list5")
+        gain_sb = load_rowvec(gain, "gain_sb", nc.sync)
+        skip_sb = load_rowvec(skip, "skip_sb", nc.sync)
+        gate1 = load_gate(wg1, 0, PACK, "gate1", nc.sync)
+        load_page(6)
+        load_page(7)
+        load_w1(0, 1)
+
+        w2_codes = held([P, H], U16, "w2_codes")
+        w2_plane = held([P, H], U8, "w2_plane")
+        deal_columns(w2_codes[:], w2_raw[:].bitcast(U16))
+        deal_columns(w2_plane[:], w2_plane_raw[:])
+        v2_plane = held([P, S], U8, "v2_plane")
+        v2_codes = held([P, S], U32, "v2_codes")
+        gather(v2_plane[:], tab2_plane[:], list2[:])
+        gather(v2_codes[:], tab2_sb[:].bitcast(U32), list2[:])
+
+        def bank(j):
+            return psum.tile([P, NB], F32, name="bank%d" % j)
+
+        def put_h2(j):
+            b, t = tiles[j]
+            cols = slice(P * j, P * (j + 1))
+            acc = bank(j)
+            nc.tensor.matmul_mx(
+                acc[:], lhsT=w2_codes[:, cols].bitcast(FP4X4), lhsT_scale=w2_plane[:, cols],
+                rhs=v2_codes[:].bitcast(FP8X4), rhs_scale=v2_plane[:], start=True, stop=True,
+            )
+            h = ring.tile([P, S], F32, name="h")
+            nc.scalar.activation(h[:], acc[:], ACT.Gelu_apprx_tanh, bias=b2_sb[:, b, t : t + 1])
+            gate = gate2_first[:, 0, :] if t == 0 else gate2_rest[:, t - 1, :]
+            nc.vector.tensor_tensor(pages[j][:].indirect(list4[:]), h[:], gate, ALU.mult)
+
+        v_plane = held([P, S], U8, "v_plane")
+        v_codes = [held([P, S], U32, "v_codes%d" % a) for a in range(K // KP)]
+        w1_codes, w1_plane = {}, {}
+
+        def quantise_w1(a, b):
+            staged = ring.tile([P, PACK * KP], BF16, name="staged", align_bytes=64)
+            nc.scalar.copy(
+                staged[:].rearrange("p (t q j) -> p q j t", t=PACK, j=PACK),
+                w1_raw[a, b][:].rearrange("p j (q t) -> p q j t", t=PACK),
+            )
+            w1_codes[a, b] = held([P, KP], U32, "w1_codes%d%d" % (a, b))
+            w1_plane[a, b] = held([P, KP], U8, "w1_plane%d%d" % (a, b))
+            nc.vector.quantize_mx(w1_codes[a, b][:].bitcast(FP8X4), w1_plane[a, b][:], staged[:])
+
+        picked = {}
+        x_staged = {}
+
+        def put_h1(j):
+            b, t = tiles[j]
+            cols = slice(P * t, P * (t + 1))
+            acc = bank(j)
+            for a in range(K // KP):
+                nc.tensor.matmul_mx(
+                    acc[:], lhsT=w1_codes[a, b][:, cols].bitcast(FP8X4), lhsT_scale=w1_plane[a, b][:, cols],
+                    rhs=v_codes[a][:].bitcast(FP8X4), rhs_scale=v_plane[4 * a :, :],
+                    start=(a == 0), stop=(a == K // KP - 1),
+                )
+            h = ring.tile([P, S], F32, name="h")
+            nc.scalar.activation(h[:], acc[:], ACT.Abs)
+            nc.vector.tensor_tensor(pages[j][:].indirect(list3[:]), h[:], gate1[:, t, :], ALU.mult)
+
+        def fetch(j):
+            b, t = tiles[j]
+            picked[j] = held([P, M], F32, "picked%d" % j)
+            if j < len(tiles) - 1:
+                gather(picked[j][:], pages[j][:], list5[:])
+            for c in range(chunks):
+                cols = slice(NB * c, NB * (c + 1))
+                if j == len(tiles) - 1:
+                    gather(picked[j][:, cols], pages[j][:], list5[:, NB // 16 * c : NB // 16 * (c + 1)])
+                if t == 0:
+                    x_staged[b, c] = ring.tile([P, PACK * NB], BF16, name="staged", align_bytes=64)
+                nc.scalar.activation(
+                    x_staged[b, c][:].rearrange("p (m t) -> p t m", t=PACK)[:, t, :],
+                    picked[j][:, cols], ACT.Copy, scale=gain_sb[:, b, t : t + 1],
+                )
+
+        x_codes, x_plane = {}, {}
+
+        def quantise_x(b, c):
+            x_codes[b, c] = held([P, NB], U32, "x_codes%d%d" % (b, c))
+            x_plane[b, c] = held([P, NB], U8, "x_plane%d%d" % (b, c))
+            nc.vector.quantize_mx(x_codes[b, c][:].bitcast(FP8X4), x_plane[b, c][:], x_staged[b, c][:])
+
+        for j in range(4):
+            put_h2(j)
+        gather(v_plane[:], tab_plane[:], list1[:])
+        for a in range(K // KP):
+            gather(v_codes[a][:], tab_sb[a][:].bitcast(U32), list1[:])
+        put_h2(4)
+        quantise_w1(0, 0)
+        put_h2(5)
+        quantise_w1(1, 0)
+        put_h2(6)
+        put_h2(7)
+
+        load_w1(1, 1)
+        w3_raw = raws.tile([P, (H // KP) * H], I32, name="raw")
+        for a in range(H // KP):
+            nc.sync.dma_start(
+                w3_raw[:, H * a : H * (a + 1)], w3_words[a].rearrange("p c i -> p (c i)").bitcast(I32)
+            )
+        load_plane(w3_plane_raw, w3_scales, nc.sync)
+        coef = held([P, H // KP, PACK], F32, "coef")
+        nc.gpsimd.tensor_tensor(coef[:], gain_sb[:], skip_sb[:], ALU.mult)
+
+        quantise_w1(0, 1)
+        quantise_w1(1, 1)
+        for j in range(4):
+            put_h1(j)
+            fetch(j)
+        w3_codes = [held([P, H], I32, "w3_codes0")]
+        w3_plane = held([P, H], U8, "w3_plane")
+        deal_columns(w3_plane[:], w3_plane_raw[:])
+        deal_columns(w3_codes[0][:], w3_raw[:, 0:H])
+        put_h1(4)
+        for c in range(chunks):
+            quantise_x(0, c)
+        for j in range(4, 8):
+            if j > 4:
+                put_h1(j)
+            fetch(j)
+        w3_codes.append(held([P, H], I32, "gate1"))
+        deal_columns(w3_codes[1][:], w3_raw[:, H : 2 * H])
+
+        for c in range(chunks):
+            quantise_x(1, c)
+            for j in range(8):
+                b, t = tiles[j]
+                cols = slice(P * j, P * (j + 1))
+                acc = bank(j)
+                for a in range(H // KP):
+                    nc.tensor.matmul_mx(
+                        acc[:], lhsT=w3_codes[a][:, cols].bitcast(FP8X4), lhsT_scale=w3_plane[4 * a :, cols],
+                        rhs=x_codes[a, c][:].bitcast(FP8X4), rhs_scale=x_plane[a, c][:],
+                        start=(a == 0), stop=(a == H // KP - 1),
+                    )
+                diff = picked[j][:, NB * c : NB * (c + 1)]
+                nc.vector.scalar_tensor_tensor(
+                    diff, diff, coef[:, b, t : t + 1], acc[:], ALU.mult, ALU.subtract
+                )
+                nc.scalar.activation(diff, diff, ACT.Square)
+                nc.sync.dma_start(out_rows[b, t, :, NB * c : NB * (c + 1)], diff)

@@ -32,8 +32,7 @@ def tile_list_throw_board_residual_kernel(
 
     with ExitStack() as ctx:
         keep = ctx.enter_context(tc.tile_pool(name="keep", bufs=1))
-        ring = ctx.enter_context(tc.tile_pool(name="ring", bufs=4))
-        raws = ctx.enter_context(tc.tile_pool(name="raws", bufs=3))
+        ring = ctx.enter_context(tc.tile_pool(name="ring", bufs=2))
         psum = ctx.enter_context(tc.psum_pool(name="psum", bufs=1))
 
         def held(shape, dtype, name):
@@ -83,10 +82,10 @@ def tile_list_throw_board_residual_kernel(
                 queue.dma_start(gate[32 * q : 32 * q + 32], rows[:, t0:t1, :])
             return gate
 
-        def deal_columns(dst, src):
+        def deal_columns(dst, src, run):
             nc.vector.tensor_copy(
-                dst.rearrange("p (b t q) -> p b q t", t=PACK, q=P),
-                src.rearrange("p (b q t) -> p b q t", t=PACK, q=P),
+                dst.rearrange("p (b t u v) -> p b u t v", t=PACK, u=P // run, v=run),
+                src.rearrange("p (b u v t) -> p b u t v", t=PACK, u=P // run, v=run),
             )
 
         def gather(dst, window, offsets):
@@ -103,11 +102,11 @@ def tile_list_throw_board_residual_kernel(
         w2_raw = held([P, H // 2], I32, "w2_raw")
         nc.sync.dma_start(w2_raw[:], w2_words[0].bitcast(I32))
         tab2_sb = load_words(tab2_words[0], "tab2_sb")
-        load_page(0)
-        load_plane(w2_plane_raw, w2_scales, nc.scalar)
-        b2_sb = load_rowvec(b2, "b2_sb", nc.scalar)
+        load_plane(w2_plane_raw, w2_scales, nc.sync)
+        b2_sb = load_rowvec(b2, "b2_sb", nc.sync)
         list4 = load_list(offs4, "list4")
-        gate2_first = load_gate(wg2, 0, 1, "gate2_first", nc.gpsimd)
+        gate2_first = load_gate(wg2, 0, 1, "gate2_first", nc.sync)
+        load_page(0)
         load_page(1)
         gate2_rest = load_gate(wg2, 1, PACK, "gate2_rest", nc.sync)
         load_page(2)
@@ -122,29 +121,26 @@ def tile_list_throw_board_residual_kernel(
 
         w1_raw = {}
 
-        def load_w1(a, b):
-            w1_raw[a, b] = raws.tile([P, PACK, KP], F32, name="raw")
+        def load_w1(a, b, slot):
+            w1_raw[a, b] = held([P, PACK, KP], F32, slot)
             nc.sync.dma_start(
                 w1_raw[a, b][:],
                 w1[KP * a : KP * (a + 1), KP * b : KP * (b + 1)].rearrange("(p j) c -> p j c", j=PACK),
             )
 
-        load_w1(0, 0)
-        load_w1(1, 0)
+        load_w1(0, 0, "raw0")
+        load_w1(1, 0, "raw1")
         load_page(5)
-        list3 = load_list(offs3, "list3")
-        list5 = load_list(offs5, "list5")
-        gain_sb = load_rowvec(gain, "gain_sb", nc.sync)
-        skip_sb = load_rowvec(skip, "skip_sb", nc.sync)
-        gate1 = load_gate(wg1, 0, PACK, "gate1", nc.sync)
         load_page(6)
         load_page(7)
-        load_w1(0, 1)
+        list3 = load_list(offs3, "list3")
+        gate1_a = load_gate(wg1, 0, 1, "gate1_a", nc.sync)
+        load_w1(0, 1, "raw2")
 
         w2_codes = held([P, H], U16, "w2_codes")
         w2_plane = held([P, H], U8, "w2_plane")
-        deal_columns(w2_codes[:], w2_raw[:].bitcast(U16))
-        deal_columns(w2_plane[:], w2_plane_raw[:])
+        deal_columns(w2_codes[:], w2_raw[:].bitcast(U16), 8)
+        deal_columns(w2_plane[:], w2_plane_raw[:], 16)
         v2_plane = held([P, S], U8, "v2_plane")
         v2_codes = held([P, S], U32, "v2_codes")
         gather(v2_plane[:], tab2_plane[:], list2[:])
@@ -161,7 +157,7 @@ def tile_list_throw_board_residual_kernel(
                 acc[:], lhsT=w2_codes[:, cols].bitcast(FP4X4), lhsT_scale=w2_plane[:, cols],
                 rhs=v2_codes[:].bitcast(FP8X4), rhs_scale=v2_plane[:], start=True, stop=True,
             )
-            h = ring.tile([P, S], F32, name="h")
+            h = ring.tile([P, S], F32, name="h2", bufs=4)
             nc.scalar.activation(h[:], acc[:], ACT.Gelu_apprx_tanh, bias=b2_sb[:, b, t : t + 1])
             gate = gate2_first[:, 0, :] if t == 0 else gate2_rest[:, t - 1, :]
             nc.vector.tensor_tensor(pages[j][:].indirect(list4[:]), h[:], gate, ALU.mult)
@@ -171,7 +167,7 @@ def tile_list_throw_board_residual_kernel(
         w1_codes, w1_plane = {}, {}
 
         def quantise_w1(a, b):
-            staged = ring.tile([P, PACK * KP], BF16, name="staged", align_bytes=64)
+            staged = held([P, PACK * KP], BF16, "stage%d%d" % (a, b))
             nc.scalar.copy(
                 staged[:].rearrange("p (t q j) -> p q j t", t=PACK, j=PACK),
                 w1_raw[a, b][:].rearrange("p j (q t) -> p q j t", t=PACK),
@@ -180,10 +176,12 @@ def tile_list_throw_board_residual_kernel(
             w1_plane[a, b] = held([P, KP], U8, "w1_plane%d%d" % (a, b))
             nc.vector.quantize_mx(w1_codes[a, b][:].bitcast(FP8X4), w1_plane[a, b][:], staged[:])
 
-        picked = {}
+        picked = [held([P, M], F32, "picked%d" % j) for j in range(len(tiles))]
         x_staged = {}
 
-        def put_h1(j):
+        h1 = {}
+
+        def make_h1(j):
             b, t = tiles[j]
             cols = slice(P * t, P * (t + 1))
             acc = bank(j)
@@ -193,30 +191,37 @@ def tile_list_throw_board_residual_kernel(
                     rhs=v_codes[a][:].bitcast(FP8X4), rhs_scale=v_plane[4 * a :, :],
                     start=(a == 0), stop=(a == K // KP - 1),
                 )
-            h = ring.tile([P, S], F32, name="h")
-            nc.scalar.activation(h[:], acc[:], ACT.Abs)
-            nc.vector.tensor_tensor(pages[j][:].indirect(list3[:]), h[:], gate1[:, t, :], ALU.mult)
+            if j < 2:
+                h1[j] = ring.tile([P, S], F32, name="h2", bufs=4)
+            else:
+                h1[j] = ring.tile([P, S], F32, name="h1")
+            nc.scalar.activation(h1[j][:], acc[:], ACT.Abs)
+
+        def put_h1(j):
+            nc.vector.tensor_tensor(pages[j][:].indirect(list3[:]), h1[j][:], gate1[tiles[j][1]], ALU.mult)
+
+        def stage_x(j, c):
+            b, t = tiles[j]
+            if t == 0:
+                x_staged[b, c] = held([P, PACK * NB], BF16, "stage%d%d" % (c, b))
+            nc.scalar.activation(
+                x_staged[b, c][:].rearrange("p (m t) -> p t m", t=PACK)[:, t, :],
+                picked[j][:, NB * c : NB * (c + 1)], ACT.Copy, scale=gain_sb[:, b, t : t + 1],
+            )
 
         def fetch(j):
-            b, t = tiles[j]
-            picked[j] = held([P, M], F32, "picked%d" % j)
-            if j < len(tiles) - 1:
-                gather(picked[j][:], pages[j][:], list5[:])
+            gather(picked[j][:], pages[j][:], list5[:])
             for c in range(chunks):
-                cols = slice(NB * c, NB * (c + 1))
-                if j == len(tiles) - 1:
-                    gather(picked[j][:, cols], pages[j][:], list5[:, NB // 16 * c : NB // 16 * (c + 1)])
-                if t == 0:
-                    x_staged[b, c] = ring.tile([P, PACK * NB], BF16, name="staged", align_bytes=64)
-                nc.scalar.activation(
-                    x_staged[b, c][:].rearrange("p (m t) -> p t m", t=PACK)[:, t, :],
-                    picked[j][:, cols], ACT.Copy, scale=gain_sb[:, b, t : t + 1],
-                )
+                stage_x(j, c)
+
+        def fetch_chunk(j, c):
+            gather(picked[j][:, NB * c : NB * (c + 1)], pages[j][:], list5[:, NB // 16 * c : NB // 16 * (c + 1)])
+            stage_x(j, c)
 
         x_codes, x_plane = {}, {}
 
         def quantise_x(b, c):
-            x_codes[b, c] = held([P, NB], U32, "x_codes%d%d" % (b, c))
+            x_codes[b, c] = held([P, NB], U32, "x_codes00" if (b, c) == (1, 1) else "x_codes%d%d" % (b, c))
             x_plane[b, c] = held([P, NB], U8, "x_plane%d%d" % (b, c))
             nc.vector.quantize_mx(x_codes[b, c][:].bitcast(FP8X4), x_plane[b, c][:], x_staged[b, c][:])
 
@@ -230,52 +235,77 @@ def tile_list_throw_board_residual_kernel(
         put_h2(5)
         quantise_w1(1, 0)
         put_h2(6)
-        put_h2(7)
 
-        load_w1(1, 1)
-        w3_raw = raws.tile([P, (H // KP) * H], I32, name="raw")
-        for a in range(H // KP):
+        load_w1(1, 1, "raw0")
+        list5 = load_list(offs5, "list5")
+        gain_sb = load_rowvec(gain, "gain_sb", nc.sync)
+        skip_sb = load_rowvec(skip, "skip_sb", nc.sync)
+        w3_raw = held([P, (H // KP) * H], I32, "raw1")
+
+        def load_w3(a):
             nc.sync.dma_start(
                 w3_raw[:, H * a : H * (a + 1)], w3_words[a].rearrange("p c i -> p (c i)").bitcast(I32)
             )
+
+        load_w3(0)
+        gate1_b = load_gate(wg1, 1, PACK, "gate1_b", nc.sync)
+        gate1 = [gate1_a[:, 0, :], gate1_b[:, 0, :], gate1_b[:, 1, :], gate1_b[:, 2, :]]
+        load_w3(1)
         load_plane(w3_plane_raw, w3_scales, nc.sync)
         coef = held([P, H // KP, PACK], F32, "coef")
         nc.gpsimd.tensor_tensor(coef[:], gain_sb[:], skip_sb[:], ALU.mult)
 
+        put_h2(7)
         quantise_w1(0, 1)
         quantise_w1(1, 1)
         for j in range(4):
+            make_h1(j)
+        for j in range(5):
             put_h1(j)
-            fetch(j)
+            if j >= 2:
+                make_h1(j + 2)
+            if j > 0:
+                fetch(j - 1)
         w3_codes = [held([P, H], I32, "w3_codes0")]
         w3_plane = held([P, H], U8, "w3_plane")
-        deal_columns(w3_plane[:], w3_plane_raw[:])
-        deal_columns(w3_codes[0][:], w3_raw[:, 0:H])
-        put_h1(4)
+        deal_columns(w3_plane[:], w3_plane_raw[:], 16)
+        deal_columns(w3_codes[0][:], w3_raw[:, 0:H], 4)
         for c in range(chunks):
             quantise_x(0, c)
-        for j in range(4, 8):
-            if j > 4:
-                put_h1(j)
-            fetch(j)
-        w3_codes.append(held([P, H], I32, "gate1"))
-        deal_columns(w3_codes[1][:], w3_raw[:, H : 2 * H])
-
+        put_h1(5)
+        make_h1(7)
+        fetch(4)
+        put_h1(6)
+        fetch(5)
+        put_h1(7)
         for c in range(chunks):
-            quantise_x(1, c)
-            for j in range(8):
-                b, t = tiles[j]
-                cols = slice(P * j, P * (j + 1))
-                acc = bank(j)
-                for a in range(H // KP):
-                    nc.tensor.matmul_mx(
-                        acc[:], lhsT=w3_codes[a][:, cols].bitcast(FP8X4), lhsT_scale=w3_plane[4 * a :, cols],
-                        rhs=x_codes[a, c][:].bitcast(FP8X4), rhs_scale=x_plane[a, c][:],
-                        start=(a == 0), stop=(a == H // KP - 1),
-                    )
-                diff = picked[j][:, NB * c : NB * (c + 1)]
-                nc.vector.scalar_tensor_tensor(
-                    diff, diff, coef[:, b, t : t + 1], acc[:], ALU.mult, ALU.subtract
+            fetch_chunk(6, c)
+            fetch_chunk(7, c)
+        w3_codes.append(held([P, H], I32, "gate1_b"))
+        deal_columns(w3_codes[1][:], w3_raw[:, H : 2 * H], 4)
+
+        def product(j, c, order):
+            cols = slice(P * j, P * (j + 1))
+            acc = bank(j)
+            for a in order:
+                nc.tensor.matmul_mx(
+                    acc[:], lhsT=w3_codes[a][:, cols].bitcast(FP8X4), lhsT_scale=w3_plane[4 * a :, cols],
+                    rhs=x_codes[a, c][:].bitcast(FP8X4), rhs_scale=x_plane[a, c][:],
+                    start=(a == order[0]), stop=(a == order[-1]),
                 )
-                nc.scalar.activation(diff, diff, ACT.Square)
-                nc.sync.dma_start(out_rows[b, t, :, NB * c : NB * (c + 1)], diff)
+            return acc
+
+        def finish(j, c, acc):
+            b, t = tiles[j]
+            diff = picked[j][:, NB * c : NB * (c + 1)]
+            nc.vector.scalar_tensor_tensor(diff, diff, coef[:, b, t : t + 1], acc[:], ALU.mult, ALU.subtract)
+            nc.scalar.activation(diff, diff, ACT.Square)
+            nc.sync.dma_start(out_rows[b, t, :, NB * c : NB * (c + 1)], diff)
+
+        quantise_x(1, 0)
+        sums = [product(j, 0, (0, 1) if j < 7 else (1, 0)) for j in range(8)]
+        quantise_x(1, 1)
+        for j in range(8):
+            finish(j, 0, sums[j])
+        for j in range(8):
+            finish(j, 1, product(j, 1, (0, 1)))

@@ -1,6 +1,7 @@
 from contextlib import ExitStack
 
 import concourse.mybir as mybir
+from concourse.masks import make_identity
 
 K, K2, H, T, S, T2, M = 1024, 512, 1024, 2048, 512, 2048, 1024
 FLOPS = 2 * (K * H * S + K2 * H * S + H * H * M)
@@ -56,10 +57,13 @@ def tile_list_throw_board_residual_kernel(
         def load_plane(plane, src, queue):
             passes = src.shape[0]
             for q in range(4):
-                queue.dma_start(
-                    plane[32 * q : 32 * q + 4 * passes, :].bitcast(I32),
-                    src[:, 4 * q : 4 * q + 4, :].bitcast(I32),
-                )
+                if passes == 1:
+                    queue.dma_start(plane[q:P:32, :].bitcast(I32), src[0, q:16:4, :].bitcast(I32))
+                else:
+                    queue.dma_start(
+                        plane[32 * q : 32 * q + 4 * passes, :].bitcast(I32),
+                        src[:, 4 * q : 4 * q + 4, :].bitcast(I32),
+                    )
 
         def load_rowvec(src, name, queue):
             vec = held([P, H // KP, PACK], F32, name)
@@ -75,11 +79,34 @@ def tile_list_throw_board_residual_kernel(
             pages[j] = held([P, T2], F32, "page%d" % j)
             nc.sync.dma_start(pages[j][:], page_rows[b, t])
 
-        def load_gate(src, t0, t1, name, queue):
-            gate = held([P, t1 - t0, S], F32, name)
-            rows = src.rearrange("(q t) s -> q t s", t=PACK)
-            for q in range(4):
-                queue.dma_start(gate[32 * q : 32 * q + 32], rows[:, t0:t1, :])
+        def bank(j):
+            return psum.tile([P, NB], F32, name="bank%d" % j)
+
+        def load_gate(src, slot):
+            rows = held([P, S], F32, slot)
+            nc.sync.dma_start(rows[:], src)
+            return rows
+
+        def turn(dst, src):
+            for c in range(S // P):
+                nc.tensor.transpose(dst[:, P * c : P * (c + 1)], src[:, P * c : P * (c + 1)], ident[:])
+
+        def turn_gate(rows, j):
+            turned = bank(j)
+            turn(turned, rows)
+            return turned
+
+        def deal_gate(turned, t, j, slot, name):
+            dealt = held([P, S], F32, slot)
+            nc.scalar.copy(
+                dealt[:].rearrange("p (c r q) -> p c r q", r=PACK, q=P // PACK),
+                turned[:].rearrange("p (c q t) -> p c q t", t=PACK, q=P // PACK)[:, :, :, t]
+                .unsqueeze(2).to_broadcast([P, S // P, PACK, P // PACK]),
+            )
+            back = bank(j)
+            turn(back, dealt)
+            gate = held([P, S], F32, name)
+            nc.scalar.copy(gate[:], back[:])
             return gate
 
         def deal_columns(dst, src, run):
@@ -93,24 +120,23 @@ def tile_list_throw_board_residual_kernel(
 
         tab2_plane = zeroed_plane(T, "tab2_plane", nc.gpsimd)
         w2_plane_raw = zeroed_plane(H, "w2_plane_raw", nc.gpsimd)
+        ident = held([P, P], F32, "ident")
+        make_identity(nc, ident[:])
         warm = held([P, 1], F32, "warm")
         nc.vector.memset(warm[:], 0.0)
         nc.scalar.activation(warm[:], warm[:], ACT.Gelu_apprx_tanh)
 
         list2 = load_list(offs2, "list2")
         load_plane(tab2_plane, tab2_scales, nc.sync)
+        wg2_rows = load_gate(wg2, "picked7")
         w2_raw = held([P, H // 2], I32, "w2_raw")
         nc.sync.dma_start(w2_raw[:], w2_words[0].bitcast(I32))
         tab2_sb = load_words(tab2_words[0], "tab2_sb")
         load_plane(w2_plane_raw, w2_scales, nc.sync)
         b2_sb = load_rowvec(b2, "b2_sb", nc.sync)
         list4 = load_list(offs4, "list4")
-        gate2_first = load_gate(wg2, 0, 1, "gate2_first", nc.sync)
-        load_page(0)
-        load_page(1)
-        gate2_rest = load_gate(wg2, 1, PACK, "gate2_rest", nc.sync)
-        load_page(2)
-        load_page(3)
+        for j in range(4):
+            load_page(j)
 
         tab_plane = zeroed_plane(T, "tab_plane", nc.vector)
         w3_plane_raw = zeroed_plane(H, "w3_plane_raw", nc.vector)
@@ -129,25 +155,23 @@ def tile_list_throw_board_residual_kernel(
             )
 
         load_w1(0, 0, "raw0")
-        load_w1(1, 0, "raw1")
         load_page(5)
+        load_w1(1, 0, "raw1")
         load_page(6)
-        load_page(7)
+        wg1_rows = load_gate(wg1, "picked6")
         list3 = load_list(offs3, "list3")
-        gate1_a = load_gate(wg1, 0, 1, "gate1_a", nc.sync)
+        load_page(7)
         load_w1(0, 1, "raw2")
 
         w2_codes = held([P, H], U16, "w2_codes")
         w2_plane = held([P, H], U8, "w2_plane")
         deal_columns(w2_codes[:], w2_raw[:].bitcast(U16), 8)
-        deal_columns(w2_plane[:], w2_plane_raw[:], 16)
         v2_plane = held([P, S], U8, "v2_plane")
         v2_codes = held([P, S], U32, "v2_codes")
         gather(v2_plane[:], tab2_plane[:], list2[:])
         gather(v2_codes[:], tab2_sb[:].bitcast(U32), list2[:])
-
-        def bank(j):
-            return psum.tile([P, NB], F32, name="bank%d" % j)
+        for b in range(H // KP):
+            deal_columns(w2_plane[:, KP * b : KP * (b + 1)], w2_plane_raw[:, KP * b : KP * (b + 1)], 16)
 
         def put_h2(j):
             b, t = tiles[j]
@@ -159,8 +183,7 @@ def tile_list_throw_board_residual_kernel(
             )
             h = ring.tile([P, S], F32, name="h2", bufs=4)
             nc.scalar.activation(h[:], acc[:], ACT.Gelu_apprx_tanh, bias=b2_sb[:, b, t : t + 1])
-            gate = gate2_first[:, 0, :] if t == 0 else gate2_rest[:, t - 1, :]
-            nc.vector.tensor_tensor(pages[j][:].indirect(list4[:]), h[:], gate, ALU.mult)
+            nc.vector.tensor_tensor(pages[j][:].indirect(list4[:]), h[:], gate2[t][:], ALU.mult)
 
         v_plane = held([P, S], U8, "v_plane")
         v_codes = [held([P, S], U32, "v_codes%d" % a) for a in range(K // KP)]
@@ -176,7 +199,6 @@ def tile_list_throw_board_residual_kernel(
             w1_plane[a, b] = held([P, KP], U8, "w1_plane%d%d" % (a, b))
             nc.vector.quantize_mx(w1_codes[a, b][:].bitcast(FP8X4), w1_plane[a, b][:], staged[:])
 
-        picked = [held([P, M], F32, "picked%d" % j) for j in range(len(tiles))]
         x_staged = {}
 
         h1 = {}
@@ -198,7 +220,7 @@ def tile_list_throw_board_residual_kernel(
             nc.scalar.activation(h1[j][:], acc[:], ACT.Abs)
 
         def put_h1(j):
-            nc.vector.tensor_tensor(pages[j][:].indirect(list3[:]), h1[j][:], gate1[tiles[j][1]], ALU.mult)
+            nc.vector.tensor_tensor(pages[j][:].indirect(list3[:]), h1[j][:], gate1[tiles[j][1]][:], ALU.mult)
 
         def stage_x(j, c):
             b, t = tiles[j]
@@ -225,8 +247,11 @@ def tile_list_throw_board_residual_kernel(
             x_plane[b, c] = held([P, NB], U8, "x_plane%d%d" % (b, c))
             nc.vector.quantize_mx(x_codes[b, c][:].bitcast(FP8X4), x_plane[b, c][:], x_staged[b, c][:])
 
-        for j in range(4):
-            put_h2(j)
+        gate2 = []
+        turned2 = turn_gate(wg2_rows, 7)
+        for t in range(PACK):
+            gate2.append(deal_gate(turned2, t, 4 + t % 3, "picked%d" % (t % 2), "gate2_%d" % t))
+            put_h2(t)
         gather(v_plane[:], tab_plane[:], list1[:])
         for a in range(K // KP):
             gather(v_codes[a][:], tab_sb[a][:].bitcast(U32), list1[:])
@@ -235,9 +260,10 @@ def tile_list_throw_board_residual_kernel(
         put_h2(5)
         quantise_w1(1, 0)
         put_h2(6)
+        turned1 = turn_gate(wg1_rows, 0)
+        gate1 = [deal_gate(turned1, t, 1 + t % 3, "picked%d" % (t % 2), "gate1_%d" % t) for t in range(PACK)]
 
         load_w1(1, 1, "raw0")
-        list5 = load_list(offs5, "list5")
         gain_sb = load_rowvec(gain, "gain_sb", nc.sync)
         skip_sb = load_rowvec(skip, "skip_sb", nc.sync)
         w3_raw = held([P, (H // KP) * H], I32, "raw1")
@@ -248,16 +274,16 @@ def tile_list_throw_board_residual_kernel(
             )
 
         load_w3(0)
-        gate1_b = load_gate(wg1, 1, PACK, "gate1_b", nc.sync)
-        gate1 = [gate1_a[:, 0, :], gate1_b[:, 0, :], gate1_b[:, 1, :], gate1_b[:, 2, :]]
         load_w3(1)
         load_plane(w3_plane_raw, w3_scales, nc.sync)
+        list5 = load_list(offs5, "list5")
         coef = held([P, H // KP, PACK], F32, "coef")
         nc.gpsimd.tensor_tensor(coef[:], gain_sb[:], skip_sb[:], ALU.mult)
 
         put_h2(7)
         quantise_w1(0, 1)
         quantise_w1(1, 1)
+        picked = [held([P, M], F32, "picked%d" % j) for j in range(len(tiles))]
         for j in range(4):
             make_h1(j)
         for j in range(5):
@@ -281,7 +307,7 @@ def tile_list_throw_board_residual_kernel(
         for c in range(chunks):
             fetch_chunk(6, c)
             fetch_chunk(7, c)
-        w3_codes.append(held([P, H], I32, "gate1_b"))
+        w3_codes.append(held([P, H], I32, "gate1_3"))
         deal_columns(w3_codes[1][:], w3_raw[:, H : 2 * H], 4)
 
         def product(j, c, order):

@@ -142,8 +142,10 @@ def tile_list_throw_board_residual_kernel(
         w3_plane_raw = zeroed_plane(H, "w3_plane_raw", nc.vector)
         list1 = load_list(offs, "list1")
         load_plane(tab_plane, tab_scales, nc.sync)
-        tab_sb = [load_words(tab_words[a], "tab_sb%d" % a) for a in range(K // KP)]
+        tab_sb = [load_words(tab_words[0], "tab_sb0")]
         load_page(4)
+        tab_sb.append(load_words(tab_words[1], "tab_sb1"))
+        load_page(5)
 
         w1_raw = {}
 
@@ -155,9 +157,8 @@ def tile_list_throw_board_residual_kernel(
             )
 
         load_w1(0, 0, "raw0")
-        load_page(5)
-        load_w1(1, 0, "raw1")
         load_page(6)
+        load_w1(1, 0, "raw1")
         wg1_rows = load_gate(wg1, "picked6")
         list3 = load_list(offs3, "list3")
         load_page(7)
@@ -199,7 +200,7 @@ def tile_list_throw_board_residual_kernel(
             w1_plane[a, b] = held([P, KP], U8, "w1_plane%d%d" % (a, b))
             nc.vector.quantize_mx(w1_codes[a, b][:].bitcast(FP8X4), w1_plane[a, b][:], staged[:])
 
-        x_staged = {}
+        x_staged, x_part = {}, {}
 
         h1 = {}
 
@@ -216,7 +217,7 @@ def tile_list_throw_board_residual_kernel(
             if j < 2:
                 h1[j] = ring.tile([P, S], F32, name="h2", bufs=4)
             else:
-                h1[j] = ring.tile([P, S], F32, name="h1")
+                h1[j] = held([P, S], F32, "h1_%d" % (j % 2))
             nc.scalar.activation(h1[j][:], acc[:], ACT.Abs)
 
         def put_h1(j):
@@ -224,20 +225,23 @@ def tile_list_throw_board_residual_kernel(
 
         def stage_x(j, c):
             b, t = tiles[j]
-            if t == 0:
-                x_staged[b, c] = held([P, PACK * NB], BF16, "stage%d%d" % (c, b))
+            if (b, c) not in x_staged:
+                slot = "raw2" if (b, c) == (1, 1) else "stage%d%d" % (c, b)
+                x_staged[b, c] = held([P, PACK * NB], BF16, slot)
             nc.scalar.activation(
                 x_staged[b, c][:].rearrange("p (m t) -> p t m", t=PACK)[:, t, :],
-                picked[j][:, NB * c : NB * (c + 1)], ACT.Copy, scale=gain_sb[:, b, t : t + 1],
+                x_part[j, c], ACT.Copy, scale=gain_sb[:, b, t : t + 1],
             )
 
-        def fetch(j):
-            gather(picked[j][:], pages[j][:], list5[:])
+        def fetch(j, slot):
+            picked = held([P, M], F32, slot)
+            gather(picked[:], pages[j][:], list5[:])
             for c in range(chunks):
-                stage_x(j, c)
+                x_part[j, c] = picked[:, NB * c : NB * (c + 1)]
 
-        def fetch_chunk(j, c):
-            gather(picked[j][:, NB * c : NB * (c + 1)], pages[j][:], list5[:, NB // 16 * c : NB // 16 * (c + 1)])
+        def fetch_chunk(j, c, slot):
+            x_part[j, c] = held([P, NB], F32, slot)[:]
+            gather(x_part[j, c], pages[j][:], list5[:, NB // 16 * c : NB // 16 * (c + 1)])
             stage_x(j, c)
 
         x_codes, x_plane = {}, {}
@@ -253,17 +257,18 @@ def tile_list_throw_board_residual_kernel(
             gate2.append(deal_gate(turned2, t, 4 + t % 3, "picked%d" % (t % 2), "gate2_%d" % t))
             put_h2(t)
         gather(v_plane[:], tab_plane[:], list1[:])
-        for a in range(K // KP):
-            gather(v_codes[a][:], tab_sb[a][:].bitcast(U32), list1[:])
+        gather(v_codes[0][:], tab_sb[0][:].bitcast(U32), list1[:])
         put_h2(4)
-        quantise_w1(0, 0)
+        gather(v_codes[1][:], tab_sb[1][:].bitcast(U32), list1[:])
         put_h2(5)
-        quantise_w1(1, 0)
+        quantise_w1(0, 0)
         put_h2(6)
+        quantise_w1(1, 0)
         turned1 = turn_gate(wg1_rows, 0)
         gate1 = [deal_gate(turned1, t, 1 + t % 3, "picked%d" % (t % 2), "gate1_%d" % t) for t in range(PACK)]
 
         load_w1(1, 1, "raw0")
+        list5 = load_list(offs5, "list5")
         gain_sb = load_rowvec(gain, "gain_sb", nc.sync)
         skip_sb = load_rowvec(skip, "skip_sb", nc.sync)
         w3_raw = held([P, (H // KP) * H], I32, "raw1")
@@ -273,40 +278,46 @@ def tile_list_throw_board_residual_kernel(
                 w3_raw[:, H * a : H * (a + 1)], w3_words[a].rearrange("p c i -> p (c i)").bitcast(I32)
             )
 
+        load_plane(w3_plane_raw, w3_scales, nc.sync)
         load_w3(0)
         load_w3(1)
-        load_plane(w3_plane_raw, w3_scales, nc.sync)
-        list5 = load_list(offs5, "list5")
         coef = held([P, H // KP, PACK], F32, "coef")
         nc.gpsimd.tensor_tensor(coef[:], gain_sb[:], skip_sb[:], ALU.mult)
 
         put_h2(7)
         quantise_w1(0, 1)
         quantise_w1(1, 1)
-        picked = [held([P, M], F32, "picked%d" % j) for j in range(len(tiles))]
         for j in range(4):
             make_h1(j)
-        for j in range(5):
+        for j in range(4):
             put_h1(j)
-            if j >= 2:
-                make_h1(j + 2)
-            if j > 0:
-                fetch(j - 1)
+        make_h1(4)
+        make_h1(5)
+        for j in (1, 2, 3, 0):
+            fetch(j, "stage11" if j == 0 else "picked%d" % j)
+            for c in range(chunks):
+                stage_x(j, c)
+        put_h1(4)
         w3_codes = [held([P, H], I32, "w3_codes0")]
         w3_plane = held([P, H], U8, "w3_plane")
         deal_columns(w3_plane[:], w3_plane_raw[:], 16)
         deal_columns(w3_codes[0][:], w3_raw[:, 0:H], 4)
         for c in range(chunks):
             quantise_x(0, c)
+        make_h1(6)
         put_h1(5)
         make_h1(7)
-        fetch(4)
-        put_h1(6)
-        fetch(5)
+        for j in (4, 5):
+            fetch(j, "picked%d" % j)
+            for c in range(chunks):
+                stage_x(j, c)
+            if j == 4:
+                put_h1(6)
+        fetch_chunk(6, 0, "picked6")
         put_h1(7)
-        for c in range(chunks):
-            fetch_chunk(6, c)
-            fetch_chunk(7, c)
+        fetch_chunk(7, 0, "picked7")
+        fetch_chunk(6, 1, "h1_1")
+        fetch_chunk(7, 1, "picked0")
         w3_codes.append(held([P, H], I32, "gate1_3"))
         deal_columns(w3_codes[1][:], w3_raw[:, H : 2 * H], 4)
 
@@ -321,17 +332,21 @@ def tile_list_throw_board_residual_kernel(
                 )
             return acc
 
-        def finish(j, c, acc):
+        def finish(j, c, acc, pieces):
             b, t = tiles[j]
-            diff = picked[j][:, NB * c : NB * (c + 1)]
-            nc.vector.scalar_tensor_tensor(diff, diff, coef[:, b, t : t + 1], acc[:], ALU.mult, ALU.subtract)
-            nc.scalar.activation(diff, diff, ACT.Square)
-            nc.sync.dma_start(out_rows[b, t, :, NB * c : NB * (c + 1)], diff)
+            width = NB // pieces
+            for m0 in range(0, NB, width):
+                diff = x_part[j, c][:, m0 : m0 + width]
+                nc.vector.scalar_tensor_tensor(
+                    diff, diff, coef[:, b, t : t + 1], acc[:, m0 : m0 + width], ALU.mult, ALU.subtract
+                )
+                nc.scalar.activation(diff, diff, ACT.Square)
+                nc.sync.dma_start(out_rows[b, t, :, NB * c + m0 : NB * c + m0 + width], diff)
 
         quantise_x(1, 0)
         sums = [product(j, 0, (0, 1) if j < 7 else (1, 0)) for j in range(8)]
         quantise_x(1, 1)
         for j in range(8):
-            finish(j, 0, sums[j])
+            finish(j, 0, sums[j], 1)
         for j in range(8):
-            finish(j, 1, product(j, 1, (0, 1)))
+            finish(j, 1, product(j, 1, (0, 1)), 2 if j == 7 else 1)

from contextlib import ExitStack

import concourse.mybir as mybir
from concourse.masks import make_identity

K, K2, H, T, S, T2, M = 1024, 512, 1024, 2048, 512, 2048, 1024
FLOPS = 2 * (K * H * S + K2 * H * S + H * H * M)

F32 = mybir.dt.float32
BF16 = mybir.dt.bfloat16
I32 = mybir.dt.int32
U32 = mybir.dt.uint32
U16 = mybir.dt.uint16
U8 = mybir.dt.uint8
FP8X4 = mybir.dt.float8_e4m3fn_x4
FP4X4 = mybir.dt.float4_e2m1fn_x4
ACT = mybir.ActivationFunctionType
ALU = mybir.AluOpType

P = 128
PACK = 4
KP = P * PACK
NB = 512


def tile_list_throw_board_residual_kernel(
    tc, tab_words, tab_scales, offs, tab2_words, tab2_scales, offs2, offs3, offs4, offs5,
    w1, w2_words, w2_scales, b2, wg1, wg2, page0, gain, w3_words, w3_scales, skip, out,
):
    nc = tc.nc
    tiles = [(b, t) for b in range(H // KP) for t in range(PACK)]
    chunks = M // NB

    with ExitStack() as ctx:
        keep = ctx.enter_context(tc.tile_pool(name="keep", bufs=1))
        ring = ctx.enter_context(tc.tile_pool(name="ring", bufs=2))
        psum = ctx.enter_context(tc.psum_pool(name="psum", bufs=1))

        def held(shape, dtype, name):
            return keep.tile(shape, dtype, name=name, align_bytes=64)

        def load_list(src, name):
            lst = held(list(src.shape), U16, name)
            nc.sync.dma_start(lst[:], src)
            return lst

        def load_words(src, name):
            words = held([P, src.shape[1]], I32, name)
            nc.sync.dma_start(words[:], src.rearrange("p c i -> p (c i)").bitcast(I32))
            return words

        def zeroed_plane(width, name, engine):
            plane = held([P, width], U8, name)
            engine.memset(plane[:].bitcast(I32), 0)
            return plane

        def load_plane(plane, src, queue):
            passes = src.shape[0]
            for q in range(4):
                if passes == 1:
                    queue.dma_start(plane[q:P:32, :].bitcast(I32), src[0, q:16:4, :].bitcast(I32))
                else:
                    queue.dma_start(
                        plane[32 * q : 32 * q + 4 * passes, :].bitcast(I32),
                        src[:, 4 * q : 4 * q + 4, :].bitcast(I32),
                    )

        def load_rowvec(src, name, queue):
            vec = held([P, H // KP, PACK], F32, name)
            queue.dma_start(vec[:], src.rearrange("(b p t) -> p b t", t=PACK, p=P))
            return vec

        page_rows = page0.rearrange("(b p t) c -> b t p c", t=PACK, p=P)
        out_rows = out.rearrange("(b p t) m -> b t p m", t=PACK, p=P)
        pages = {}

        def load_page(j):
            b, t = tiles[j]
            pages[j] = held([P, T2], F32, "page%d" % j)
            nc.sync.dma_start(pages[j][:], page_rows[b, t])

        def bank(j):
            return psum.tile([P, NB], F32, name="bank%d" % j)

        def load_gate(src, slot):
            rows = held([P, S], F32, slot)
            nc.sync.dma_start(rows[:], src)
            return rows

        def turn(dst, src):
            for c in range(S // P):
                nc.tensor.transpose(dst[:, P * c : P * (c + 1)], src[:, P * c : P * (c + 1)], ident[:])

        def turn_gate(rows, j):
            turned = bank(j)
            turn(turned, rows)
            return turned

        def deal_gate(turned, t, j, slot, name):
            dealt = held([P, S], F32, slot)
            nc.scalar.copy(
                dealt[:].rearrange("p (c r q) -> p c r q", r=PACK, q=P // PACK),
                turned[:].rearrange("p (c q t) -> p c q t", t=PACK, q=P // PACK)[:, :, :, t]
                .unsqueeze(2).to_broadcast([P, S // P, PACK, P // PACK]),
            )
            back = bank(j)
            turn(back, dealt)
            gate = held([P, S], F32, name)
            nc.scalar.copy(gate[:], back[:])
            return gate

        def deal_columns(dst, src, run):
            nc.vector.tensor_copy(
                dst.rearrange("p (b t u v) -> p b u t v", t=PACK, u=P // run, v=run),
                src.rearrange("p (b u v t) -> p b u t v", t=PACK, u=P // run, v=run),
            )

        def gather(dst, window, offsets):
            nc.vector.tensor_copy(dst, window.indirect(offsets))

        tab2_plane = zeroed_plane(T, "tab2_plane", nc.gpsimd)
        w2_plane_raw = zeroed_plane(H, "w2_plane_raw", nc.gpsimd)
        ident = held([P, P], F32, "ident")
        make_identity(nc, ident[:])
        warm = held([P, 1], F32, "warm")
        nc.vector.memset(warm[:], 0.0)
        nc.scalar.activation(warm[:], warm[:], ACT.Gelu_apprx_tanh)

        list2 = load_list(offs2, "list2")
        load_plane(tab2_plane, tab2_scales, nc.sync)
        wg2_rows = load_gate(wg2, "picked7")
        w2_raw = held([P, H // 2], I32, "w2_raw")
        nc.sync.dma_start(w2_raw[:], w2_words[0].bitcast(I32))
        tab2_sb = load_words(tab2_words[0], "tab2_sb")
        load_plane(w2_plane_raw, w2_scales, nc.sync)
        b2_sb = load_rowvec(b2, "b2_sb", nc.sync)
        list4 = load_list(offs4, "list4")
        for j in range(4):
            load_page(j)

        tab_plane = zeroed_plane(T, "tab_plane", nc.vector)
        w3_plane_raw = zeroed_plane(H, "w3_plane_raw", nc.vector)
        list1 = load_list(offs, "list1")
        load_plane(tab_plane, tab_scales, nc.sync)
        tab_sb = [load_words(tab_words[0], "tab_sb0")]
        load_page(4)
        tab_sb.append(load_words(tab_words[1], "tab_sb1"))
        load_page(5)

        w1_raw = {}

        def load_w1(a, b, slot):
            w1_raw[a, b] = held([P, PACK, KP], F32, slot)
            nc.sync.dma_start(
                w1_raw[a, b][:],
                w1[KP * a : KP * (a + 1), KP * b : KP * (b + 1)].rearrange("(p j) c -> p j c", j=PACK),
            )

        load_w1(0, 0, "raw0")
        load_page(6)
        load_w1(1, 0, "raw1")
        wg1_rows = load_gate(wg1, "picked6")
        list3 = load_list(offs3, "list3")
        load_page(7)
        load_w1(0, 1, "raw2")

        w2_codes = held([P, H], U16, "w2_codes")
        w2_plane = held([P, H], U8, "w2_plane")
        deal_columns(w2_codes[:], w2_raw[:].bitcast(U16), 8)
        v2_plane = held([P, S], U8, "v2_plane")
        v2_codes = held([P, S], U32, "v2_codes")
        gather(v2_plane[:], tab2_plane[:], list2[:])
        gather(v2_codes[:], tab2_sb[:].bitcast(U32), list2[:])
        for b in range(H // KP):
            deal_columns(w2_plane[:, KP * b : KP * (b + 1)], w2_plane_raw[:, KP * b : KP * (b + 1)], 16)

        def put_h2(j):
            b, t = tiles[j]
            cols = slice(P * j, P * (j + 1))
            acc = bank(j)
            nc.tensor.matmul_mx(
                acc[:], lhsT=w2_codes[:, cols].bitcast(FP4X4), lhsT_scale=w2_plane[:, cols],
                rhs=v2_codes[:].bitcast(FP8X4), rhs_scale=v2_plane[:], start=True, stop=True,
            )
            h = ring.tile([P, S], F32, name="h2", bufs=4)
            nc.scalar.activation(h[:], acc[:], ACT.Gelu_apprx_tanh, bias=b2_sb[:, b, t : t + 1])
            nc.vector.tensor_tensor(pages[j][:].indirect(list4[:]), h[:], gate2[t][:], ALU.mult)

        v_plane = held([P, S], U8, "v_plane")
        v_codes = [held([P, S], U32, "v_codes%d" % a) for a in range(K // KP)]
        w1_codes, w1_plane = {}, {}

        def quantise_w1(a, b):
            staged = held([P, PACK * KP], BF16, "stage%d%d" % (a, b))
            nc.scalar.copy(
                staged[:].rearrange("p (t q j) -> p q j t", t=PACK, j=PACK),
                w1_raw[a, b][:].rearrange("p j (q t) -> p q j t", t=PACK),
            )
            w1_codes[a, b] = held([P, KP], U32, "w1_codes%d%d" % (a, b))
            w1_plane[a, b] = held([P, KP], U8, "w1_plane%d%d" % (a, b))
            nc.vector.quantize_mx(w1_codes[a, b][:].bitcast(FP8X4), w1_plane[a, b][:], staged[:])

        x_staged, x_part = {}, {}

        h1 = {}

        def make_h1(j):
            b, t = tiles[j]
            cols = slice(P * t, P * (t + 1))
            acc = bank(j)
            for a in range(K // KP):
                nc.tensor.matmul_mx(
                    acc[:], lhsT=w1_codes[a, b][:, cols].bitcast(FP8X4), lhsT_scale=w1_plane[a, b][:, cols],
                    rhs=v_codes[a][:].bitcast(FP8X4), rhs_scale=v_plane[4 * a :, :],
                    start=(a == 0), stop=(a == K // KP - 1),
                )
            if j < 2:
                h1[j] = ring.tile([P, S], F32, name="h2", bufs=4)
            else:
                h1[j] = held([P, S], F32, "h1_%d" % (j % 2))
            nc.scalar.activation(h1[j][:], acc[:], ACT.Abs)

        def put_h1(j):
            nc.vector.tensor_tensor(pages[j][:].indirect(list3[:]), h1[j][:], gate1[tiles[j][1]][:], ALU.mult)

        def stage_x(j, c):
            b, t = tiles[j]
            if (b, c) not in x_staged:
                slot = "raw2" if (b, c) == (1, 1) else "stage%d%d" % (c, b)
                x_staged[b, c] = held([P, PACK * NB], BF16, slot)
            nc.scalar.activation(
                x_staged[b, c][:].rearrange("p (m t) -> p t m", t=PACK)[:, t, :],
                x_part[j, c], ACT.Copy, scale=gain_sb[:, b, t : t + 1],
            )

        def fetch(j, slot):
            picked = held([P, M], F32, slot)
            gather(picked[:], pages[j][:], list5[:])
            for c in range(chunks):
                x_part[j, c] = picked[:, NB * c : NB * (c + 1)]

        def fetch_chunk(j, c, slot):
            x_part[j, c] = held([P, NB], F32, slot)[:]
            gather(x_part[j, c], pages[j][:], list5[:, NB // 16 * c : NB // 16 * (c + 1)])
            stage_x(j, c)

        x_codes, x_plane = {}, {}

        def quantise_x(b, c):
            x_codes[b, c] = held([P, NB], U32, "x_codes00" if (b, c) == (1, 1) else "x_codes%d%d" % (b, c))
            x_plane[b, c] = held([P, NB], U8, "x_plane%d%d" % (b, c))
            nc.vector.quantize_mx(x_codes[b, c][:].bitcast(FP8X4), x_plane[b, c][:], x_staged[b, c][:])

        gate2 = []
        turned2 = turn_gate(wg2_rows, 7)
        for t in range(PACK):
            gate2.append(deal_gate(turned2, t, 4 + t % 3, "picked%d" % (t % 2), "gate2_%d" % t))
            put_h2(t)
        gather(v_plane[:], tab_plane[:], list1[:])
        gather(v_codes[0][:], tab_sb[0][:].bitcast(U32), list1[:])
        put_h2(4)
        gather(v_codes[1][:], tab_sb[1][:].bitcast(U32), list1[:])
        put_h2(5)
        quantise_w1(0, 0)
        put_h2(6)
        quantise_w1(1, 0)
        turned1 = turn_gate(wg1_rows, 0)
        gate1 = [deal_gate(turned1, t, 1 + t % 3, "picked%d" % (t % 2), "gate1_%d" % t) for t in range(PACK)]

        load_w1(1, 1, "raw0")
        list5 = load_list(offs5, "list5")
        gain_sb = load_rowvec(gain, "gain_sb", nc.sync)
        skip_sb = load_rowvec(skip, "skip_sb", nc.sync)
        w3_raw = held([P, (H // KP) * H], I32, "raw1")

        def load_w3(a):
            nc.sync.dma_start(
                w3_raw[:, H * a : H * (a + 1)], w3_words[a].rearrange("p c i -> p (c i)").bitcast(I32)
            )

        load_plane(w3_plane_raw, w3_scales, nc.sync)
        load_w3(0)
        load_w3(1)
        coef = held([P, H // KP, PACK], F32, "coef")
        nc.gpsimd.tensor_tensor(coef[:], gain_sb[:], skip_sb[:], ALU.mult)

        put_h2(7)
        quantise_w1(0, 1)
        quantise_w1(1, 1)
        for j in range(4):
            make_h1(j)
        for j in range(4):
            put_h1(j)
        make_h1(4)
        make_h1(5)
        for j in (1, 2, 3, 0):
            fetch(j, "stage11" if j == 0 else "picked%d" % j)
            for c in range(chunks):
                stage_x(j, c)
        put_h1(4)
        w3_codes = [held([P, H], I32, "w3_codes0")]
        w3_plane = held([P, H], U8, "w3_plane")
        deal_columns(w3_plane[:], w3_plane_raw[:], 16)
        deal_columns(w3_codes[0][:], w3_raw[:, 0:H], 4)
        for c in range(chunks):
            quantise_x(0, c)
        make_h1(6)
        put_h1(5)
        make_h1(7)
        for j in (4, 5):
            fetch(j, "picked%d" % j)
            for c in range(chunks):
                stage_x(j, c)
            if j == 4:
                put_h1(6)
        fetch_chunk(6, 0, "picked6")
        put_h1(7)
        fetch_chunk(7, 0, "picked7")
        fetch_chunk(6, 1, "h1_1")
        fetch_chunk(7, 1, "picked0")
        w3_codes.append(held([P, H], I32, "gate1_3"))
        deal_columns(w3_codes[1][:], w3_raw[:, H : 2 * H], 4)

        def product(j, c, order):
            cols = slice(P * j, P * (j + 1))
            acc = bank(j)
            for a in order:
                nc.tensor.matmul_mx(
                    acc[:], lhsT=w3_codes[a][:, cols].bitcast(FP8X4), lhsT_scale=w3_plane[4 * a :, cols],
                    rhs=x_codes[a, c][:].bitcast(FP8X4), rhs_scale=x_plane[a, c][:],
                    start=(a == order[0]), stop=(a == order[-1]),
                )
            return acc

        def finish(j, c, acc, pieces):
            b, t = tiles[j]
            width = NB // pieces
            for m0 in range(0, NB, width):
                diff = x_part[j, c][:, m0 : m0 + width]
                nc.vector.scalar_tensor_tensor(
                    diff, diff, coef[:, b, t : t + 1], acc[:, m0 : m0 + width], ALU.mult, ALU.subtract
                )
                nc.scalar.activation(diff, diff, ACT.Square)
                nc.sync.dma_start(out_rows[b, t, :, NB * c + m0 : NB * c + m0 + width], diff)

        quantise_x(1, 0)
        sums = [product(j, 0, (0, 1) if j < 7 else (1, 0)) for j in range(8)]
        quantise_x(1, 1)
        for j in range(8):
            finish(j, 0, sums[j], 1)
        for j in range(8):
            finish(j, 1, product(j, 1, (0, 1)), 2 if j == 7 else 1)
